import numpy as np
import ml_dtypes

BF16 = ml_dtypes.bfloat16


def bf(x):
    return np.asarray(x, np.float32).astype(BF16)


def f32(x):
    return np.asarray(x, np.float32)


def f64(x):
    return np.asarray(x).astype(np.float64)


def striped(idx):
    return np.tile(idx.reshape(-1, 16).T, (8, 1))


S, K, M, N, E, Q = 256, 512, 256, 192, 2, 96


def setup_inputs():
    return {"base": bf(np.random.standard_normal((M, S))), "x": bf(np.random.standard_normal((K, N))), "w": bf(np.random.standard_normal((E, K, M)) / np.sqrt(K)), "b": f32(0.5 * np.random.standard_normal((M, 1))), "offs": striped(np.random.permutation(S)[:N])}


def reference(base, x, w, b, offs):
    idx = offs[:16].T.reshape(-1)
    z = f64(base).copy()
    for e in range(E):
        z[:, idx[e * Q : (e + 1) * Q]] += f64(w)[e].T @ f64(x)[:, e * Q : (e + 1) * Q]
    return z + f64(b)

@@ -1,0 +1,63 @@
+import concourse.mybir as mybir
+from concourse.masks import make_identity
+
+BF16, F32, U16 = mybir.dt.bfloat16, mybir.dt.float32, mybir.dt.uint16
+
+P = 128
+TOKENS = 256
+K = 512
+M = 256
+N = 192
+EXPERTS = 2
+PIECE = N // EXPERTS
+PIECE_COLS = PIECE // 16
+K_BLOCKS = K // P
+M_BLOCKS = M // P
+
+FLOPS = 2 * K * M * N
+
+
+def tile_scatter_matmul_kernel(tc, base, x, w, b, offs, out):
+    nc = tc.nc
+    with (
+        tc.tile_pool(name="held", bufs=1) as held,
+        tc.psum_pool(name="banks", bufs=1) as banks,
+    ):
+        offsets = held.tile([P, N // 16], U16, name="offsets")
+        nc.sync.dma_start(offsets[:], offs)
+
+        base_sb = held.tile([P, M_BLOCKS, TOKENS], BF16, name="base_sb")
+        nc.scalar.dma_start(base_sb[:], base.rearrange("(a p) t -> p a t", p=P))
+
+        bias = held.tile([P, M_BLOCKS], F32, name="bias")
+        nc.scalar.dma_start(bias[:], b.rearrange("(a p) o -> p (a o)", p=P))
+
+        x_sb = held.tile([P, K_BLOCKS, N], BF16, name="x_sb")
+        nc.sync.dma_start(x_sb[:], x.rearrange("(c p) j -> p c j", p=P))
+
+        w_sb = [held.tile([P, K_BLOCKS, M], BF16, name="w_sb%d" % e) for e in range(EXPERTS)]
+        nc.sync.dma_start(w_sb[0][:], w[0].rearrange("(c p) m -> p c m", p=P))
+        nc.scalar.dma_start(w_sb[1][:], w[1].rearrange("(c p) m -> p c m", p=P))
+
+        identity = held.tile([P, P], BF16, name="identity")
+        make_identity(nc, identity[:])
+
+        windows = [banks.tile([P, TOKENS], F32, name="window%d" % a) for a in range(M_BLOCKS)]
+        for a in range(M_BLOCKS):
+            nc.tensor.matmul(windows[a][:], identity[:], base_sb[:, a, :], start=True, stop=False)
+
+        for a in range(M_BLOCKS):
+            for e in range(EXPERTS):
+                piece = offsets[:, e * PIECE_COLS : (e + 1) * PIECE_COLS]
+                for c in range(K_BLOCKS):
+                    nc.tensor.matmul(
+                        windows[a][:].indirect(piece),
+                        w_sb[e][:, c, a * P : (a + 1) * P],
+                        x_sb[:, c, e * PIECE : (e + 1) * PIECE],
+                        start=False,
+                        stop=(e == EXPERTS - 1 and c == K_BLOCKS - 1),
+                    )
+
+            z = held.tile([P, TOKENS], F32, name="z%d" % a)
+            nc.vector.tensor_scalar_add(z[:], windows[a][:], bias[:, a : a + 1])
+            nc.sync.dma_start(out[a * P : (a + 1) * P, :], z[:])

@@ -13,6 +13,10 @@ PIECE = N // EXPERTS
 PIECE_COLS = PIECE // 16
 K_BLOCKS = K // P
 M_BLOCKS = M // P
+C_PER_LOAD = 2
+LOADS = K_BLOCKS // C_PER_LOAD
+BANK = 512
+WARM_MATMULS = 4
 
 FLOPS = 2 * K * M * N
 
@@ -29,35 +33,48 @@ def tile_scatter_matmul_kernel(tc, base, x, w, b, offs, out):
         base_sb = held.tile([P, M_BLOCKS, TOKENS], BF16, name="base_sb")
         nc.scalar.dma_start(base_sb[:], base.rearrange("(a p) t -> p a t", p=P))
 
-        bias = held.tile([P, M_BLOCKS], F32, name="bias")
-        nc.scalar.dma_start(bias[:], b.rearrange("(a p) o -> p (a o)", p=P))
-
         x_sb = held.tile([P, K_BLOCKS, N], BF16, name="x_sb")
         nc.sync.dma_start(x_sb[:], x.rearrange("(c p) j -> p c j", p=P))
 
-        w_sb = [held.tile([P, K_BLOCKS, M], BF16, name="w_sb%d" % e) for e in range(EXPERTS)]
-        nc.sync.dma_start(w_sb[0][:], w[0].rearrange("(c p) m -> p c m", p=P))
-        nc.scalar.dma_start(w_sb[1][:], w[1].rearrange("(c p) m -> p c m", p=P))
+        queues = (nc.scalar, nc.sync)
+        w_sb = [[None] * LOADS for e in range(EXPERTS)]
+        for e in range(EXPERTS):
+            w_blocks = w[e].rearrange("(c p) m -> p c m", p=P)
+            for h in range(LOADS):
+                w_sb[e][h] = held.tile([P, C_PER_LOAD, M], BF16, name="w_sb%d%d" % (e, h))
+                queues[h % 2].dma_start(
+                    w_sb[e][h][:], w_blocks[:, h * C_PER_LOAD : (h + 1) * C_PER_LOAD, :]
+                )
 
         identity = held.tile([P, P], BF16, name="identity")
         make_identity(nc, identity[:])
+
+        bias = held.tile([P, M_BLOCKS], F32, name="bias")
+        nc.scalar.dma_start(bias[:], b.rearrange("(a p) o -> p (a o)", p=P))
+
+        zeros = held.tile([P, BANK], BF16, name="zeros")
+        nc.vector.memset(zeros[:], 0.0)
+        unused = banks.tile([P, BANK], F32, name="unused")
+        for i in range(WARM_MATMULS):
+            nc.tensor.matmul(unused[:], zeros[:, 0:P], zeros[:], start=True, stop=True)
 
         windows = [banks.tile([P, TOKENS], F32, name="window%d" % a) for a in range(M_BLOCKS)]
         for a in range(M_BLOCKS):
             nc.tensor.matmul(windows[a][:], identity[:], base_sb[:, a, :], start=True, stop=False)
 
-        for a in range(M_BLOCKS):
-            for e in range(EXPERTS):
-                piece = offsets[:, e * PIECE_COLS : (e + 1) * PIECE_COLS]
+        for e in range(EXPERTS):
+            piece = offsets[:, e * PIECE_COLS : (e + 1) * PIECE_COLS]
+            for a in range(M_BLOCKS):
                 for c in range(K_BLOCKS):
                     nc.tensor.matmul(
                         windows[a][:].indirect(piece),
-                        w_sb[e][:, c, a * P : (a + 1) * P],
+                        w_sb[e][c // C_PER_LOAD][:, c % C_PER_LOAD, a * P : (a + 1) * P],
                         x_sb[:, c, e * PIECE : (e + 1) * PIECE],
                         start=False,
                         stop=(e == EXPERTS - 1 and c == K_BLOCKS - 1),
                     )
 
+        for a in range(M_BLOCKS):
             z = held.tile([P, TOKENS], F32, name="z%d" % a)
             nc.vector.tensor_scalar_add(z[:], windows[a][:], bias[:, a : a + 1])
-            nc.sync.dma_start(out[a * P : (a + 1) * P, :], z[:])
+            queues[a % 2].dma_start(out[a * P : (a + 1) * P, :], z[:])

@@ -15,8 +15,6 @@ K_BLOCKS = K // P
 M_BLOCKS = M // P
 C_PER_LOAD = 2
 LOADS = K_BLOCKS // C_PER_LOAD
-BANK = 512
-WARM_MATMULS = 4
 
 FLOPS = 2 * K * M * N
 
@@ -51,12 +49,6 @@ def tile_scatter_matmul_kernel(tc, base, x, w, b, offs, out):
 
         bias = held.tile([P, M_BLOCKS], F32, name="bias")
         nc.scalar.dma_start(bias[:], b.rearrange("(a p) o -> p (a o)", p=P))
-
-        zeros = held.tile([P, BANK], BF16, name="zeros")
-        nc.vector.memset(zeros[:], 0.0)
-        unused = banks.tile([P, BANK], F32, name="unused")
-        for i in range(WARM_MATMULS):
-            nc.tensor.matmul(unused[:], zeros[:, 0:P], zeros[:], start=True, stop=True)
 
         windows = [banks.tile([P, TOKENS], F32, name="window%d" % a) for a in range(M_BLOCKS)]
         for a in range(M_BLOCKS):

@@ -15,6 +15,8 @@ K_BLOCKS = K // P
 M_BLOCKS = M // P
 C_PER_LOAD = 2
 LOADS = K_BLOCKS // C_PER_LOAD
+BANK = 512
+WARM_MATMULS = 4
 
 FLOPS = 2 * K * M * N
 
@@ -32,12 +34,12 @@ def tile_scatter_matmul_kernel(tc, base, x, w, b, offs, out):
         nc.scalar.dma_start(base_sb[:], base.rearrange("(a p) t -> p a t", p=P))
 
         x_sb = held.tile([P, K_BLOCKS, N], BF16, name="x_sb")
-        nc.sync.dma_start(x_sb[:], x.rearrange("(c p) j -> p c j", p=P))
+        nc.sync.dma_start(x_sb[:], x.rearrange("(p c) j -> p c j", p=P))
 
         queues = (nc.scalar, nc.sync)
         w_sb = [[None] * LOADS for e in range(EXPERTS)]
         for e in range(EXPERTS):
-            w_blocks = w[e].rearrange("(c p) m -> p c m", p=P)
+            w_blocks = w[e].rearrange("(p c) m -> p c m", p=P)
             for h in range(LOADS):
                 w_sb[e][h] = held.tile([P, C_PER_LOAD, M], BF16, name="w_sb%d%d" % (e, h))
                 queues[h % 2].dma_start(
@@ -49,6 +51,12 @@ def tile_scatter_matmul_kernel(tc, base, x, w, b, offs, out):
 
         bias = held.tile([P, M_BLOCKS], F32, name="bias")
         nc.scalar.dma_start(bias[:], b.rearrange("(a p) o -> p (a o)", p=P))
+
+        zeros = held.tile([P, BANK], BF16, name="zeros")
+        nc.vector.memset(zeros[:], 0.0)
+        unused = banks.tile([P, BANK], F32, name="unused")
+        for i in range(WARM_MATMULS):
+            nc.tensor.matmul(unused[:], zeros[:, 0:P], zeros[:], start=True, stop=True)
 
         windows = [banks.tile([P, TOKENS], F32, name="window%d" % a) for a in range(M_BLOCKS)]
         for a in range(M_BLOCKS):

@@ -31,26 +31,27 @@ def tile_scatter_matmul_kernel(tc, base, x, w, b, offs, out):
         nc.sync.dma_start(offsets[:], offs)
 
         base_sb = held.tile([P, M_BLOCKS, TOKENS], BF16, name="base_sb")
-        nc.scalar.dma_start(base_sb[:], base.rearrange("(a p) t -> p a t", p=P))
+        nc.sync.dma_start(base_sb[:], base.rearrange("(a p) t -> p a t", p=P))
 
-        x_sb = held.tile([P, K_BLOCKS, N], BF16, name="x_sb")
-        nc.sync.dma_start(x_sb[:], x.rearrange("(p c) j -> p c j", p=P))
-
-        queues = (nc.scalar, nc.sync)
-        w_sb = [[None] * LOADS for e in range(EXPERTS)]
+        x_blocks = x.rearrange("(p c) j -> p c j", p=P)
+        x_sb = [held.tile([P, C_PER_LOAD, N], BF16, name="x_sb%d" % h) for h in range(LOADS)]
+        w_sb = [
+            [held.tile([P, C_PER_LOAD, M], BF16, name="w_sb%d%d" % (e, h)) for h in range(LOADS)]
+            for e in range(EXPERTS)
+        ]
         for e in range(EXPERTS):
             w_blocks = w[e].rearrange("(p c) m -> p c m", p=P)
             for h in range(LOADS):
-                w_sb[e][h] = held.tile([P, C_PER_LOAD, M], BF16, name="w_sb%d%d" % (e, h))
-                queues[h % 2].dma_start(
-                    w_sb[e][h][:], w_blocks[:, h * C_PER_LOAD : (h + 1) * C_PER_LOAD, :]
-                )
+                blocks = slice(h * C_PER_LOAD, (h + 1) * C_PER_LOAD)
+                if e == 0:
+                    nc.sync.dma_start(x_sb[h][:], x_blocks[:, blocks, :])
+                nc.sync.dma_start(w_sb[e][h][:], w_blocks[:, blocks, :])
+
+        bias = held.tile([P, M_BLOCKS], F32, name="bias")
+        nc.sync.dma_start(bias[:], b.rearrange("(a p) o -> p (a o)", p=P))
 
         identity = held.tile([P, P], BF16, name="identity")
         make_identity(nc, identity[:])
-
-        bias = held.tile([P, M_BLOCKS], F32, name="bias")
-        nc.scalar.dma_start(bias[:], b.rearrange("(a p) o -> p (a o)", p=P))
 
         zeros = held.tile([P, BANK], BF16, name="zeros")
         nc.vector.memset(zeros[:], 0.0)
@@ -64,16 +65,18 @@ def tile_scatter_matmul_kernel(tc, base, x, w, b, offs, out):
 
         for e in range(EXPERTS):
             piece = offsets[:, e * PIECE_COLS : (e + 1) * PIECE_COLS]
-            for a in range(M_BLOCKS):
-                for c in range(K_BLOCKS):
-                    nc.tensor.matmul(
-                        windows[a][:].indirect(piece),
-                        w_sb[e][c // C_PER_LOAD][:, c % C_PER_LOAD, a * P : (a + 1) * P],
-                        x_sb[:, c, e * PIECE : (e + 1) * PIECE],
-                        start=False,
-                        stop=(e == EXPERTS - 1 and c == K_BLOCKS - 1),
-                    )
+            for h in range(LOADS):
+                for a in range(M_BLOCKS):
+                    for i in range(C_PER_LOAD):
+                        nc.tensor.matmul(
+                            windows[a][:].indirect(piece),
+                            w_sb[e][h][:, i, a * P : (a + 1) * P],
+                            x_sb[h][:, i, e * PIECE : (e + 1) * PIECE],
+                            start=False,
+                            stop=(e == EXPERTS - 1 and h == LOADS - 1 and i == C_PER_LOAD - 1),
+                        )
 
+        queues = (nc.scalar, nc.sync)
         for a in range(M_BLOCKS):
             z = held.tile([P, TOKENS], F32, name="z%d" % a)
             nc.vector.tensor_scalar_add(z[:], windows[a][:], bias[:, a : a + 1])

@@ -16,7 +16,7 @@ M_BLOCKS = M // P
 C_PER_LOAD = 2
 LOADS = K_BLOCKS // C_PER_LOAD
 BANK = 512
-WARM_MATMULS = 4
+WARM_MATMULS = 3
 
 FLOPS = 2 * K * M * N
 

@@ -13,7 +13,7 @@ PIECE = N // EXPERTS
 PIECE_COLS = PIECE // 16
 K_BLOCKS = K // P
 M_BLOCKS = M // P
-C_PER_LOAD = 2
+C_PER_LOAD = 1
 LOADS = K_BLOCKS // C_PER_LOAD
 BANK = 512
 WARM_MATMULS = 3
@@ -34,18 +34,17 @@ def tile_scatter_matmul_kernel(tc, base, x, w, b, offs, out):
         nc.sync.dma_start(base_sb[:], base.rearrange("(a p) t -> p a t", p=P))
 
         x_blocks = x.rearrange("(p c) j -> p c j", p=P)
+        w_blocks = [w[e].rearrange("(p c) m -> p c m", p=P) for e in range(EXPERTS)]
         x_sb = [held.tile([P, C_PER_LOAD, N], BF16, name="x_sb%d" % h) for h in range(LOADS)]
         w_sb = [
             [held.tile([P, C_PER_LOAD, M], BF16, name="w_sb%d%d" % (e, h)) for h in range(LOADS)]
             for e in range(EXPERTS)
         ]
-        for e in range(EXPERTS):
-            w_blocks = w[e].rearrange("(p c) m -> p c m", p=P)
-            for h in range(LOADS):
-                blocks = slice(h * C_PER_LOAD, (h + 1) * C_PER_LOAD)
-                if e == 0:
-                    nc.sync.dma_start(x_sb[h][:], x_blocks[:, blocks, :])
-                nc.sync.dma_start(w_sb[e][h][:], w_blocks[:, blocks, :])
+        for h in range(LOADS):
+            blocks = slice(h * C_PER_LOAD, (h + 1) * C_PER_LOAD)
+            nc.sync.dma_start(x_sb[h][:], x_blocks[:, blocks, :])
+            for e in range(EXPERTS):
+                nc.sync.dma_start(w_sb[e][h][:], w_blocks[e][:, blocks, :])
 
         bias = held.tile([P, M_BLOCKS], F32, name="bias")
         nc.sync.dma_start(bias[:], b.rearrange("(a p) o -> p (a o)", p=P))
@@ -63,17 +62,16 @@ def tile_scatter_matmul_kernel(tc, base, x, w, b, offs, out):
         for a in range(M_BLOCKS):
             nc.tensor.matmul(windows[a][:], identity[:], base_sb[:, a, :], start=True, stop=False)
 
-        for e in range(EXPERTS):
-            piece = offsets[:, e * PIECE_COLS : (e + 1) * PIECE_COLS]
-            for h in range(LOADS):
-                for a in range(M_BLOCKS):
+        for h in range(LOADS):
+            for a in range(M_BLOCKS):
+                for e in range(EXPERTS):
                     for i in range(C_PER_LOAD):
                         nc.tensor.matmul(
-                            windows[a][:].indirect(piece),
+                            windows[a][:].indirect(offsets[:, e * PIECE_COLS : (e + 1) * PIECE_COLS]),
                             w_sb[e][h][:, i, a * P : (a + 1) * P],
                             x_sb[h][:, i, e * PIECE : (e + 1) * PIECE],
                             start=False,
-                            stop=(e == EXPERTS - 1 and h == LOADS - 1 and i == C_PER_LOAD - 1),
+                            stop=(h == LOADS - 1 and e == EXPERTS - 1 and i == C_PER_LOAD - 1),
                         )
 
         queues = (nc.scalar, nc.sync)

@@ -13,7 +13,7 @@ PIECE = N // EXPERTS
 PIECE_COLS = PIECE // 16
 K_BLOCKS = K // P
 M_BLOCKS = M // P
-C_PER_LOAD = 1
+C_PER_LOAD = 2
 LOADS = K_BLOCKS // C_PER_LOAD
 BANK = 512
 WARM_MATMULS = 3

@@ -74,8 +74,7 @@ def tile_scatter_matmul_kernel(tc, base, x, w, b, offs, out):
                             stop=(h == LOADS - 1 and e == EXPERTS - 1 and i == C_PER_LOAD - 1),
                         )
 
-        queues = (nc.scalar, nc.sync)
         for a in range(M_BLOCKS):
             z = held.tile([P, TOKENS], F32, name="z%d" % a)
             nc.vector.tensor_scalar_add(z[:], windows[a][:], bias[:, a : a + 1])
-            queues[a % 2].dma_start(out[a * P : (a + 1) * P, :], z[:])
+            nc.sync.dma_start(out[a * P : (a + 1) * P, :], z[:])

@@ -63,16 +63,19 @@ def tile_scatter_matmul_kernel(tc, base, x, w, b, offs, out):
             nc.tensor.matmul(windows[a][:], identity[:], base_sb[:, a, :], start=True, stop=False)
 
         for h in range(LOADS):
-            for a in range(M_BLOCKS):
-                for e in range(EXPERTS):
-                    for i in range(C_PER_LOAD):
-                        nc.tensor.matmul(
-                            windows[a][:].indirect(offsets[:, e * PIECE_COLS : (e + 1) * PIECE_COLS]),
-                            w_sb[e][h][:, i, a * P : (a + 1) * P],
-                            x_sb[h][:, i, e * PIECE : (e + 1) * PIECE],
-                            start=False,
-                            stop=(h == LOADS - 1 and e == EXPERTS - 1 and i == C_PER_LOAD - 1),
-                        )
+            if h == LOADS - 1:
+                order = [(a, e) for a in range(M_BLOCKS) for e in range(EXPERTS)]
+            else:
+                order = [(a, e) for e in range(EXPERTS) for a in range(M_BLOCKS)]
+            for a, e in order:
+                for i in range(C_PER_LOAD):
+                    nc.tensor.matmul(
+                        windows[a][:].indirect(offsets[:, e * PIECE_COLS : (e + 1) * PIECE_COLS]),
+                        w_sb[e][h][:, i, a * P : (a + 1) * P],
+                        x_sb[h][:, i, e * PIECE : (e + 1) * PIECE],
+                        start=False,
+                        stop=(h == LOADS - 1 and e == EXPERTS - 1 and i == C_PER_LOAD - 1),
+                    )
 
         for a in range(M_BLOCKS):
             z = held.tile([P, TOKENS], F32, name="z%d" % a)

@@ -33,18 +33,17 @@ def tile_scatter_matmul_kernel(tc, base, x, w, b, offs, out):
         base_sb = held.tile([P, M_BLOCKS, TOKENS], BF16, name="base_sb")
         nc.sync.dma_start(base_sb[:], base.rearrange("(a p) t -> p a t", p=P))
 
-        x_blocks = x.rearrange("(p c) j -> p c j", p=P)
-        w_blocks = [w[e].rearrange("(p c) m -> p c m", p=P) for e in range(EXPERTS)]
+        x_steps = x.rearrange("(h p i) j -> h p i j", h=LOADS, p=P)
+        w_steps = [w[e].rearrange("(h p i) m -> h p i m", h=LOADS, p=P) for e in range(EXPERTS)]
         x_sb = [held.tile([P, C_PER_LOAD, N], BF16, name="x_sb%d" % h) for h in range(LOADS)]
         w_sb = [
             [held.tile([P, C_PER_LOAD, M], BF16, name="w_sb%d%d" % (e, h)) for h in range(LOADS)]
             for e in range(EXPERTS)
         ]
         for h in range(LOADS):
-            blocks = slice(h * C_PER_LOAD, (h + 1) * C_PER_LOAD)
-            nc.sync.dma_start(x_sb[h][:], x_blocks[:, blocks, :])
+            nc.sync.dma_start(x_sb[h][:], x_steps[h])
             for e in range(EXPERTS):
-                nc.sync.dma_start(w_sb[e][h][:], w_blocks[e][:, blocks, :])
+                nc.sync.dma_start(w_sb[e][h][:], w_steps[e][h])
 
         bias = held.tile([P, M_BLOCKS], F32, name="bias")
         nc.sync.dma_start(bias[:], b.rearrange("(a p) o -> p (a o)", p=P))

@@ -48,11 +48,13 @@ def tile_scatter_matmul_kernel(tc, base, x, w, b, offs, out):
         bias = held.tile([P, M_BLOCKS], F32, name="bias")
         nc.sync.dma_start(bias[:], b.rearrange("(a p) o -> p (a o)", p=P))
 
-        identity = held.tile([P, P], BF16, name="identity")
-        make_identity(nc, identity[:])
-
         zeros = held.tile([P, BANK], BF16, name="zeros")
         nc.vector.memset(zeros[:], 0.0)
+
+        identity = held.tile([P, P], BF16, name="identity")
+        nc.vector.memset(identity[:], 0.0)
+        make_identity(nc, identity[:], nomemset=True)
+
         unused = banks.tile([P, BANK], F32, name="unused")
         for i in range(WARM_MATMULS):
             nc.tensor.matmul(unused[:], zeros[:, 0:P], zeros[:], start=True, stop=True)

@@ -15,8 +15,7 @@ K_BLOCKS = K // P
 M_BLOCKS = M // P
 C_PER_LOAD = 2
 LOADS = K_BLOCKS // C_PER_LOAD
-BANK = 512
-WARM_MATMULS = 3
+WARM_MATMULS = 12
 
 FLOPS = 2 * K * M * N
 
@@ -48,16 +47,16 @@ def tile_scatter_matmul_kernel(tc, base, x, w, b, offs, out):
         bias = held.tile([P, M_BLOCKS], F32, name="bias")
         nc.sync.dma_start(bias[:], b.rearrange("(a p) o -> p (a o)", p=P))
 
-        zeros = held.tile([P, BANK], BF16, name="zeros")
+        zeros = held.tile([P, P], BF16, name="zeros")
         nc.vector.memset(zeros[:], 0.0)
 
         identity = held.tile([P, P], BF16, name="identity")
         nc.vector.memset(identity[:], 0.0)
         make_identity(nc, identity[:], nomemset=True)
 
-        unused = banks.tile([P, BANK], F32, name="unused")
+        unused = banks.tile([P, P], F32, name="unused")
         for i in range(WARM_MATMULS):
-            nc.tensor.matmul(unused[:], zeros[:, 0:P], zeros[:], start=True, stop=True)
+            nc.tensor.matmul(unused[:], zeros[:], zeros[:], start=True, stop=True)
 
         windows = [banks.tile([P, TOKENS], F32, name="window%d" % a) for a in range(M_BLOCKS)]
         for a in range(M_BLOCKS):

@@ -15,6 +15,7 @@ K_BLOCKS = K // P
 M_BLOCKS = M // P
 C_PER_LOAD = 2
 LOADS = K_BLOCKS // C_PER_LOAD
+SQUARE = 32
 WARM_MATMULS = 12
 
 FLOPS = 2 * K * M * N
@@ -44,15 +45,20 @@ def tile_scatter_matmul_kernel(tc, base, x, w, b, offs, out):
             for e in range(EXPERTS):
                 nc.sync.dma_start(w_sb[e][h][:], w_steps[e][h])
 
-        bias = held.tile([P, M_BLOCKS], F32, name="bias")
-        nc.sync.dma_start(bias[:], b.rearrange("(a p) o -> p (a o)", p=P))
-
         zeros = held.tile([P, P], BF16, name="zeros")
         nc.vector.memset(zeros[:], 0.0)
 
         identity = held.tile([P, P], BF16, name="identity")
         nc.vector.memset(identity[:], 0.0)
         make_identity(nc, identity[:], nomemset=True)
+
+        bias_rows = held.tile([P, SQUARE], F32, name="bias_rows", align_bytes=64)
+        nc.vector.memset(bias_rows[:], 0.0)
+        b_rows = b.rearrange("(a g r) o -> a g (r o)", a=M_BLOCKS, r=SQUARE)
+        for a in range(M_BLOCKS):
+            nc.sync.dma_start(bias_rows[a:P:SQUARE, :], b_rows[a])
+        bias = held.tile([P, SQUARE], F32, name="bias", align_bytes=64)
+        nc.vector.transpose(bias[:], bias_rows[:])
 
         unused = banks.tile([P, P], F32, name="unused")
         for i in range(WARM_MATMULS):

@@ -15,6 +15,7 @@ K_BLOCKS = K // P
 M_BLOCKS = M // P
 C_PER_LOAD = 2
 LOADS = K_BLOCKS // C_PER_LOAD
+HALVES = 2
 SQUARE = 32
 WARM_MATMULS = 12
 
@@ -83,7 +84,10 @@ def tile_scatter_matmul_kernel(tc, base, x, w, b, offs, out):
                         stop=(h == LOADS - 1 and e == EXPERTS - 1 and i == C_PER_LOAD - 1),
                     )
 
+        piece = TOKENS // HALVES
         for a in range(M_BLOCKS):
             z = held.tile([P, TOKENS], F32, name="z%d" % a)
-            nc.vector.tensor_scalar_add(z[:], windows[a][:], bias[:, a : a + 1])
-            nc.sync.dma_start(out[a * P : (a + 1) * P, :], z[:])
+            for c in range(HALVES):
+                cols = slice(c * piece, (c + 1) * piece)
+                nc.vector.tensor_scalar_add(z[:, cols], windows[a][:, cols], bias[:, a : a + 1])
+                nc.sync.dma_start(out[a * P : (a + 1) * P, cols], z[:, cols])

import concourse.mybir as mybir
from concourse.masks import make_identity

BF16, F32, U16 = mybir.dt.bfloat16, mybir.dt.float32, mybir.dt.uint16

P = 128
TOKENS = 256
K = 512
M = 256
N = 192
EXPERTS = 2
PIECE = N // EXPERTS
PIECE_COLS = PIECE // 16
K_BLOCKS = K // P
M_BLOCKS = M // P
C_PER_LOAD = 2
LOADS = K_BLOCKS // C_PER_LOAD
HALVES = 2
SQUARE = 32
WARM_MATMULS = 12

FLOPS = 2 * K * M * N


def tile_scatter_matmul_kernel(tc, base, x, w, b, offs, out):
    nc = tc.nc
    with (
        tc.tile_pool(name="held", bufs=1) as held,
        tc.psum_pool(name="banks", bufs=1) as banks,
    ):
        offsets = held.tile([P, N // 16], U16, name="offsets")
        nc.sync.dma_start(offsets[:], offs)

        base_sb = held.tile([P, M_BLOCKS, TOKENS], BF16, name="base_sb")
        nc.sync.dma_start(base_sb[:], base.rearrange("(a p) t -> p a t", p=P))

        x_steps = x.rearrange("(h p i) j -> h p i j", h=LOADS, p=P)
        w_steps = [w[e].rearrange("(h p i) m -> h p i m", h=LOADS, p=P) for e in range(EXPERTS)]
        x_sb = [held.tile([P, C_PER_LOAD, N], BF16, name="x_sb%d" % h) for h in range(LOADS)]
        w_sb = [
            [held.tile([P, C_PER_LOAD, M], BF16, name="w_sb%d%d" % (e, h)) for h in range(LOADS)]
            for e in range(EXPERTS)
        ]
        for h in range(LOADS):
            nc.sync.dma_start(x_sb[h][:], x_steps[h])
            for e in range(EXPERTS):
                nc.sync.dma_start(w_sb[e][h][:], w_steps[e][h])

        zeros = held.tile([P, P], BF16, name="zeros")
        nc.vector.memset(zeros[:], 0.0)

        identity = held.tile([P, P], BF16, name="identity")
        nc.vector.memset(identity[:], 0.0)
        make_identity(nc, identity[:], nomemset=True)

        bias_rows = held.tile([P, SQUARE], F32, name="bias_rows", align_bytes=64)
        nc.vector.memset(bias_rows[:], 0.0)
        b_rows = b.rearrange("(a g r) o -> a g (r o)", a=M_BLOCKS, r=SQUARE)
        for a in range(M_BLOCKS):
            nc.sync.dma_start(bias_rows[a:P:SQUARE, :], b_rows[a])
        bias = held.tile([P, SQUARE], F32, name="bias", align_bytes=64)
        nc.vector.transpose(bias[:], bias_rows[:])

        unused = banks.tile([P, P], F32, name="unused")
        for i in range(WARM_MATMULS):
            nc.tensor.matmul(unused[:], zeros[:], zeros[:], start=True, stop=True)

        windows = [banks.tile([P, TOKENS], F32, name="window%d" % a) for a in range(M_BLOCKS)]
        for a in range(M_BLOCKS):
            nc.tensor.matmul(windows[a][:], identity[:], base_sb[:, a, :], start=True, stop=False)

        for h in range(LOADS):
            if h == LOADS - 1:
                order = [(a, e) for a in range(M_BLOCKS) for e in range(EXPERTS)]
            else:
                order = [(a, e) for e in range(EXPERTS) for a in range(M_BLOCKS)]
            for a, e in order:
                for i in range(C_PER_LOAD):
                    nc.tensor.matmul(
                        windows[a][:].indirect(offsets[:, e * PIECE_COLS : (e + 1) * PIECE_COLS]),
                        w_sb[e][h][:, i, a * P : (a + 1) * P],
                        x_sb[h][:, i, e * PIECE : (e + 1) * PIECE],
                        start=False,
                        stop=(h == LOADS - 1 and e == EXPERTS - 1 and i == C_PER_LOAD - 1),
                    )

        piece = TOKENS // HALVES
        for a in range(M_BLOCKS):
            z = held.tile([P, TOKENS], F32, name="z%d" % a)
            for c in range(HALVES):
                cols = slice(c * piece, (c + 1) * piece)
                nc.vector.tensor_scalar_add(z[:, cols], windows[a][:, cols], bias[:, a : a + 1])
                nc.sync.dma_start(out[a * P : (a + 1) * P, cols], z[:, cols])
